import numpy as np
import ml_dtypes


def mxq(x, axis, fmt="e4m3"):
    dtype, down = {"e4m3": (ml_dtypes.float8_e4m3fn, 7), "e5m2": (ml_dtypes.float8_e5m2, 14)}[fmt]
    v = np.moveaxis(np.asarray(x, np.float32).astype(ml_dtypes.bfloat16).astype(np.float64), axis, -1)
    blocks = v.reshape(v.shape[:-1] + (-1, 32))
    amax = np.abs(blocks).max(-1, keepdims=True)
    byte = np.maximum(np.where(amax > 0, np.frexp(amax)[1] - 1 + 127, 0) - down, 1)
    scale = np.exp2(byte - 127.0)
    codes = (blocks / scale).astype(np.float32).astype(dtype).astype(np.float64)
    return np.moveaxis((codes * scale).reshape(v.shape), -1, axis)


WIDE = False


def mx_kscale(k):
    if not WIDE:
        return np.ones(k)
    levels = np.array([10, -10, 5, -5, 0])
    if k % 512:
        return np.exp2(np.random.permutation(np.resize(levels, k // 32))).repeat(32)
    a = np.empty((k // 512, 16))
    for p in range(k // 512):
        a[p, :8] = np.random.permutation(np.resize(levels, 8))
        for g in range(8):
            far = levels[np.abs(levels - a[p, g]) >= 10]
            a[p, g + 8] = far[np.random.randint(len(far))]
    return np.exp2(a.ravel()).repeat(32)


BF16 = ml_dtypes.bfloat16


def bf(x):
    return np.asarray(x, np.float32).astype(BF16)


def f64(x):
    return np.asarray(x).astype(np.float64)


NO, NV, S, B = 512, 1024, 2, 1024
CORR = 0.4


def setup_inputs():
    s, t, u = mx_kscale(B), mx_kscale(B), mx_kscale(NV)
    s2, t2 = np.tile(s, S), np.tile(t, S)
    return {"vir": bf(np.random.standard_normal((NV, S * B)) * s2 * u[:, None]),
            "n": bf((1 + 0.1 * np.random.standard_normal(B)) / s * t),
            "d": bf(CORR * np.random.standard_normal((B, B)) / np.sqrt(B) / s[:, None] * t),
            "occ": bf(np.random.standard_normal((NO, S * B)) * t2),
            "mix": bf(CORR * np.random.standard_normal((NO, NV)) / np.sqrt(NV) / u),
            "gain": bf((1 + 0.1 * np.random.standard_normal(S * B)) / t2),
            "e_ba": bf(CORR * np.random.standard_normal((B, B)) / np.sqrt(B) / t[:, None]),
            "e_ab": bf(CORR * np.random.standard_normal((B, B)) / np.sqrt(B) / t[:, None])}


def reference(vir, n, d, occ, mix, gain, e_ba, e_ab):
    v = f64(vir).reshape(NV * S, B)
    p = mxq(v, 1, "e4m3") @ mxq(f64(d), 0, "e4m3")
    v1 = (v * f64(n) + p).reshape(NV, S * B)
    o1 = f64(occ) + (mxq(f64(mix), 1, "e4m3") @ mxq(v1, 0, "e4m3"))
    q = mxq(o1, 1, "e4m3")
    r = o1 * f64(gain)
    alpha = r[:, :B] + (q[:, B:] @ mxq(f64(e_ba), 0, "e4m3"))
    beta = r[:, B:] + (q[:, :B] @ mxq(f64(e_ab), 0, "e4m3"))
    return alpha, beta

from contextlib import ExitStack

import concourse.mybir as mybir
from concourse.masks import make_identity

NO, NV, S, B = 512, 1024, 2, 1024
FLOPS = 2 * (NV * S * B * B + NO * NV * S * B + 2 * NO * B * B)

F32 = mybir.dt.float32
BF16 = mybir.dt.bfloat16
U32 = mybir.dt.uint32
U8 = mybir.dt.uint8
FP8X4 = mybir.dt.float8_e4m3fn_x4
ADD = mybir.AluOpType.add
MULT = mybir.AluOpType.mult

P = 128
H = 512


def tile_orbital_mixing_spin_exchange_t1_kernel(tc, vir, n, d, occ, mix, gain, e_ba, e_ab, out_0, out_1):
    nc = tc.nc
    outs = (out_0, out_1)
    e_dram = (e_ab, e_ba)

    with ExitStack() as ctx:
        const = ctx.enter_context(tc.tile_pool(name="const", bufs=1))
        sb = ctx.enter_context(tc.tile_pool(name="sb", bufs=2))
        psum = ctx.enter_context(tc.psum_pool(name="psum", bufs=8))

        def bank(name):
            return psum.tile([P, H], F32, name=name, tag="bank", bufs=8)

        nat = {}
        raw = {}
        occs = {}

        def load_rows(key, src):
            t = sb.tile([P, 4 * H], BF16, name="nat", tag="nat", bufs=5, align_bytes=64)
            nc.sync.dma_start(out=t[:].rearrange("p (a c) -> p a c", a=4), in_=src.rearrange("(a p) c -> p a c", p=P))
            nat[key] = t

        def load_vir(s, vh, g):
            load_rows((s, vh, g), vir[H * vh:H * (vh + 1), B * s + H * g:B * s + H * (g + 1)])

        def load_mix(g):
            load_rows(("mix", g), mix[:, H * g:H * (g + 1)])

        def load_k(key, src):
            t = sb.tile([P, 4 * H], BF16, name="raw", tag="raw", bufs=5, align_bytes=64)
            nc.sync.dma_start(out=t[:].rearrange("p (j c) -> p j c", j=4), in_=src.rearrange("(p j) c -> p j c", j=4))
            raw[key] = t

        def load_d(h, g):
            load_k(("d", h, g), d[H * g:H * (g + 1), H * h:H * (h + 1)])

        def load_e(s, h, half):
            load_k(("e", s, h, half), e_dram[s][H * h:H * (h + 1), H * half:H * (half + 1)])

        def load_occ(G):
            s, h = G // 2, G % 2
            t = sb.tile([P, 4 * H], BF16, name="occt", tag="occ", bufs=3, align_bytes=64)
            nc.sync.dma_start(
                out=t[:].rearrange("p (a c) -> p a c", a=4),
                in_=occ[:, B * s + H * h:B * s + H * (h + 1)].rearrange("(a p) c -> p a c", p=P),
            )
            occs[G] = t

        ident = const.tile([P, P], F32, name="ident")
        perm = const.tile([P, P], F32, name="perm")
        n_bf = const.tile([P, 8], BF16, name="n_bf")
        n_sb = const.tile([P, 8], F32, name="n_sb")
        gain_sb = const.tile([P, S * B], BF16, name="gain_sb", align_bytes=64)
        make_identity(nc, ident[:])
        nc.vector.tensor_copy(
            out=perm[:].rearrange("p (u q e) -> p u q e", u=2, e=2),
            in_=ident[:].rearrange("p (q u e) -> p u q e", u=2, e=2),
        )

        virT, vq, mixT, mixq = {}, {}, {}, {}
        kgrp, dq, eq = {}, {}, {}
        v1T, v1g, v1q, o1, o1b, o1g, qq = {}, {}, {}, {}, {}, {}, {}

        def codes(tag, width, bufs):
            c = sb.tile([P, width], U32, name=tag + "_c", tag=tag + "_c", bufs=bufs, align_bytes=64)
            sc = sb.tile([P, width], U8, name=tag + "_s", tag=tag + "_s", bufs=bufs, align_bytes=64)
            return c, sc

        def quant(cs, lo, width, src):
            nc.vector.quantize_mx(
                out=cs[0][:, lo:lo + width].bitcast(FP8X4), scales=cs[1][:, lo:lo + width], in_=src)

        def mm(out, l, lo, r, ro, n_cols, start, stop):
            nc.tensor.matmul_mx(
                out=out,
                lhsT=l[0][:, lo:lo + P].bitcast(FP8X4), lhsT_scale=l[1][:, lo:lo + P],
                rhs=r[0][:, ro:ro + n_cols].bitcast(FP8X4), rhs_scale=r[1][:, ro:ro + n_cols],
                start=start, stop=stop)

        def T_vir(s, vh, g, b):
            if (s, g) not in virT:
                virT[s, g] = sb.tile([P, 4 * NV], BF16, name="virT", tag="virT", bufs=3, align_bytes=64)
            src = nat[s, vh, g][:].bitcast(F32)
            ps = bank("tv")
            for a2 in range(2):
                a = 2 * b + a2
                for w in range(2):
                    nc.tensor.transpose(ps[:, (2 * a2 + w) * P:(2 * a2 + w + 1) * P],
                                        src[:, 256 * a + w:256 * (a + 1):2], perm[:])
            for u in range(2):
                lo = 2048 * vh + 1024 * u + 512 * b
                nc.scalar.copy(
                    out=virT[s, g][:, lo:lo + 512].bitcast(F32).rearrange("p (a x w) -> p a x w", a=2, w=2),
                    in_=ps[:].rearrange("p (a w u x) -> p u a x w", a=2, w=2, u=2)[:, u])

        def Q_vir(s, vh, g):
            if (s, g) not in vq:
                vq[s, g] = codes("vq", NV, 4)
            quant(vq[s, g], H * vh, H, virT[s, g][:, 2048 * vh:2048 * (vh + 1)])

        def T_mix(g, b):
            if g not in mixT:
                mixT[g] = sb.tile([P, 2048], BF16, name="mixT", tag="kgrp", bufs=3, align_bytes=64)
            src = nat["mix", g][:].bitcast(F32)
            ps = bank("tm")
            for a2 in range(2):
                a = 2 * b + a2
                for w in range(2):
                    nc.tensor.transpose(ps[:, (2 * a2 + w) * P:(2 * a2 + w + 1) * P],
                                        src[:, 256 * a + w:256 * (a + 1):2], ident[:])
            nc.scalar.copy(
                out=mixT[g][:, 1024 * b:1024 * (b + 1)].bitcast(F32).rearrange("p (a x w) -> p a x w", a=2, w=2),
                in_=ps[:].rearrange("p (a w x) -> p a x w", a=2, w=2))

        def Q_mix(g):
            mixq[g] = codes("mixq", NO, 2)
            quant(mixq[g], 0, NO, mixT[g][:])

        def copy(eng, out, in_):
            if eng == "v":
                nc.vector.tensor_copy(out=out, in_=in_)
            else:
                nc.scalar.copy(out=out, in_=in_)

        def I_d(h, g, i, eng):
            if i == 0:
                kgrp["d", h, g] = sb.tile([P, 2048], BF16, name="kgrp", tag="kgrp", bufs=3, align_bytes=64)
            copy(eng,
                 kgrp["d", h, g][:, 1024 * i:1024 * (i + 1)].rearrange("p (t m j) -> p t m j", t=2, j=4),
                 raw["d", h, g][:].rearrange("p (j m t) -> p t m j", j=4, t=4)[:, 2 * i:2 * i + 2])

        def Q_d(h, g):
            dq[h, g] = codes("dq", H, 4)
            quant(dq[h, g], 0, H, kgrp["d", h, g][:])

        def I_e(s, h, half, i, eng):
            if eng == "g":
                if i == 0:
                    kgrp["e", s, h, half] = sb.tile([P, 2048], BF16, name="kgrp", tag="kgrp", bufs=3, align_bytes=64)
                nc.gpsimd.tensor_scalar(
                    out=kgrp["e", s, h, half][:, 1024 * i:1024 * (i + 1)].rearrange("p (c j) -> p c j", j=4),
                    in0=raw["e", s, h, half][:].rearrange("p (j c) -> p c j", j=4)[:, 256 * i:256 * (i + 1)],
                    scalar1=1.0, scalar2=0.0, op0=MULT, op1=ADD)
                return
            if i == 0:
                kgrp["e", s, h, half] = sb.tile([P, 2048], BF16, name="kgrp", tag="kgrp", bufs=3, align_bytes=64)
            copy(eng,
                 kgrp["e", s, h, half][:, 1024 * i:1024 * (i + 1)].rearrange("p (c j) -> p c j", j=4),
                 raw["e", s, h, half][:].rearrange("p (j c) -> p c j", j=4)[:, 256 * i:256 * (i + 1)])

        def Q_e(s, h, half):
            eq[s, h, half] = codes("eq", H, 8)
            quant(eq[s, h, half], 0, H, kgrp["e", s, h, half][:])

        def P1(k, t):
            G, vh = k // 2, k % 2
            s, h = G // 2, G % 2
            ps = bank("p1")
            for g in range(2):
                mm(ps[:], dq[h, g], P * t, vq[s, g], H * vh, H, g == 0, g == 1)
            v1T[k, t] = sb.tile([P, H], BF16, name="v1T", tag="v1T", bufs=6, align_bytes=64)
            nc.vector.scalar_tensor_tensor(
                out=v1T[k, t][:],
                in0=virT[s, h][:, 2048 * vh:2048 * (vh + 1)].rearrange("p (v j) -> p v j", j=4)[:, :, t],
                scalar=n_sb[:, 4 * h + t:4 * h + t + 1],
                in1=ps[:], op0=MULT, op1=ADD)

        def T_v1(k, tp, eng="a"):
            if tp == 0:
                v1g[k] = sb.tile([P, 2048], BF16, name="v1g", tag="v1g", bufs=2, align_bytes=64)
            ps = bank("t1")
            for t2 in range(2):
                src = v1T[k, 2 * tp + t2][:].bitcast(F32)
                for u in range(2):
                    nc.tensor.transpose(ps[:, (2 * t2 + u) * P:(2 * t2 + u + 1) * P], src[:, P * u:P * (u + 1)], ident[:])
            copy(eng,
                out=v1g[k][:, 1024 * tp:1024 * (tp + 1)].bitcast(F32).rearrange("p (m t u) -> p m t u", t=2, u=2),
                in_=ps[:].rearrange("p (t u m) -> p m t u", t=2, u=2))

        def Q_v1(k):
            v1q[k] = codes("v1q", H, 4)
            quant(v1q[k], 0, H, v1g[k][:])

        def P2(G, a):
            s, h = G // 2, G % 2
            ps = bank("p2")
            for vh in range(2):
                mm(ps[:], mixq[vh], P * a, v1q[2 * G + vh], 0, H, vh == 0, vh == 1)
            o1[G, a] = sb.tile([P, H], F32, name="o1", tag="o1", bufs=16, align_bytes=64)
            nc.vector.tensor_tensor(
                out=o1[G, a][:].rearrange("p (u m e) -> p u m e", u=2, e=2),
                in0=ps[:].rearrange("p (u m e) -> p u m e", u=2, e=2),
                in1=occs[G][:, H * a:H * (a + 1)].rearrange("p (m u e) -> p u m e", u=2, e=2), op=ADD)

        def B_o1(G, a, eng):
            o1b[G, a] = sb.tile([P, H], BF16, name="o1b", tag="o1b", bufs=4, align_bytes=64)
            if eng == "g":
                nc.gpsimd.tensor_scalar(out=o1b[G, a][:], in0=o1[G, a][:], scalar1=1.0, scalar2=0.0, op0=MULT, op1=ADD)
            else:
                copy(eng, o1b[G, a][:], o1[G, a][:])

        def T_o1(G, i):
            if i == 0:
                o1g[G] = sb.tile([P, 2048], BF16, name="o1g", tag="o1g", bufs=2, align_bytes=64)
            ps = bank("t2")
            for a2 in range(2):
                src = o1b[G, 2 * i + a2][:].bitcast(F32)
                for u in range(2):
                    nc.tensor.transpose(ps[:, (2 * a2 + u) * P:(2 * a2 + u + 1) * P], src[:, P * u:P * (u + 1)], ident[:])
            nc.scalar.copy(
                out=o1g[G][:, 1024 * i:1024 * (i + 1)].bitcast(F32).rearrange("p (a o u) -> p a o u", a=2, u=2),
                in_=ps[:].rearrange("p (a u o) -> p a o u", a=2, u=2))

        def R(G, a):
            s, h = G // 2, G % 2
            nc.gpsimd.tensor_tensor(
                out=o1[G, a][:].rearrange("p (u m e) -> p u m e", u=2, e=2),
                in0=o1[G, a][:].rearrange("p (u m e) -> p u m e", u=2, e=2),
                in1=gain_sb[:, B * s + H * h:B * s + H * (h + 1)].rearrange("p (m u e) -> p u m e", u=2, e=2), op=MULT)

        def Q_o1(G, lo, cnt):
            if lo == 0:
                qq[G] = codes("qq", NO, 4)
            quant(qq[G], P * lo, P * cnt, o1g[G][:, H * lo:H * (lo + cnt)])

        def P3(s, a, half):
            ps = bank("p3")
            for h in range(2):
                mm(ps[:], qq[2 * (1 - s) + h], P * a, eq[1 - s, h, half], 0, H, h == 0, h == 1)
            res = sb.tile([P, H], F32, name="res", tag="res", bufs=6, align_bytes=64)
            nc.vector.tensor_tensor(
                out=res[:].rearrange("p (m u e) -> p m u e", u=2, e=2),
                in0=ps[:].rearrange("p (m u e) -> p m u e", u=2, e=2),
                in1=o1[2 * s + half, a][:].rearrange("p (u m e) -> p m u e", u=2, e=2), op=ADD)
            nc.sync.dma_start(out=outs[s][P * a:P * (a + 1), H * half:H * (half + 1)], in_=res[:])

        load_vir(0, 0, 0)
        load_d(0, 0)
        load_vir(0, 0, 1)
        load_d(0, 1)
        nc.scalar.dma_start(out=n_bf[:].rearrange("p (h t) -> p h t", h=2), in_=n.rearrange("(h m t) -> m h t", h=2, t=4))
        load_vir(0, 1, 0)
        load_vir(0, 1, 1)
        for g in range(2):
            load_d(1, g)

        ctx.enter_context(tc.manual_schedule())
        T_vir(0, 0, 0, 0)
        T_vir(0, 0, 0, 1)
        I_d(0, 0, 0, "v")
        I_d(0, 0, 1, "v")
        Q_vir(0, 0, 0)
        T_vir(0, 0, 1, 0)
        T_vir(0, 0, 1, 1)
        Q_d(0, 0)
        I_d(0, 1, 0, "v")
        I_d(0, 1, 1, "a")
        Q_vir(0, 0, 1)
        Q_d(0, 1)
        nc.vector.tensor_copy(out=n_sb[:], in_=n_bf[:])
        load_mix(0)

        def P2s(G, al, eng="g"):
            for a in al:
                P2(G, a)
                if eng == "g":
                    B_o1(G, a, eng)
            for a in al:
                if eng != "g":
                    B_o1(G, a, eng)
            for a in al:
                R(G, a)

        for g in range(2):
            T_vir(0, 1, g, 0)
            T_vir(0, 1, g, 1)
        load_mix(1)
        for t in range(4):
            P1(0, t)
        Q_vir(0, 1, 0)
        Q_vir(0, 1, 1)
        for g in range(2):
            for i in range(2):
                I_d(1, g, i, "a")
        load_vir(1, 0, 0)
        load_vir(1, 0, 1)
        T_v1(0, 0)
        Q_d(1, 0)
        Q_d(1, 1)
        for g in range(2):
            T_mix(g, 0)
            T_mix(g, 1)
        load_vir(1, 1, 0)
        load_occ(0)
        load_vir(1, 1, 1)
        nc.sync.dma_start(out=gain_sb[:], in_=gain.partition_broadcast(P))
        T_v1(0, 1)
        for t in range(4):
            P1(1, t)
        Q_v1(0)
        Q_mix(0)
        Q_mix(1)
        for half in range(2):
            for h in range(2):
                load_e(0, h, half)
            if half == 0:
                load_occ(1)
        T_v1(1, 0)
        for g in range(2):
            T_vir(1, 0, g, 0)
            T_vir(1, 0, g, 1)
        T_v1(1, 1)
        for t in range(4):
            P1(2, t)
        Q_v1(1)
        Q_vir(1, 0, 0)
        Q_vir(1, 0, 1)
        ea = [(0, h, half, i) for half in range(2) for h in range(2) for i in range(2)]
        eb = [(1, h, half, i) for half in range(2) for h in range(2) for i in range(2)]

        def e_work(lst, cnt, eng="a"):
            for x in range(cnt):
                if not lst:
                    return
                it = lst[0]
                lst.remove(it)
                I_e(it[0], it[1], it[2], it[3], eng)
                if it[3] == 1:
                    pend.append(it[:3])

        pend = []

        def e_quant():
            for it in pend:
                Q_e(*it)
            pend.clear()

        T_v1(2, 0)
        for g in range(2):
            T_vir(1, 1, g, 0)
            T_vir(1, 1, g, 1)
        T_v1(2, 1)
        load_occ(2)
        load_e(1, 0, 0)
        P2s(0, (0, 1))
        for t in range(4):
            P1(3, t)
        Q_v1(2)
        Q_vir(1, 1, 0)
        Q_vir(1, 1, 1)
        e_work(ea, 2, "g")
        e_work(ea, 2)

        def unit(k, g_o1, i_o1, g_p2, a_p2, ew, p3a=(), p3b=()):
            T_v1(k - 1, 0)
            T_o1(g_o1, i_o1)
            T_v1(k - 1, 1)
            P2s(g_p2, a_p2)
            for it in p3a:
                P3(*it)
            for t in range(4):
                P1(k, t)
            Q_v1(k - 1)
            Q_o1(g_o1, 2 * i_o1, 2)
            e_quant()
            for it in p3b:
                P3(*it)
            e_work(*ew)

        load_e(1, 1, 0)
        unit(4, 0, 0, 0, (2, 3), (ea, 2))
        load_occ(3)
        load_e(1, 0, 1)
        unit(5, 0, 1, 1, (0, 1), (ea, 2))
        load_e(1, 1, 1)
        unit(6, 1, 0, 1, (2, 3), (eb, 2))
        unit(7, 1, 1, 2, (0, 1), (eb, 2))
        T_v1(7, 0)
        T_o1(2, 0)
        T_v1(7, 1, "v")
        P2s(2, (2, 3))
        Q_v1(7)
        P3(1, 0, 0)
        P3(1, 1, 0)
        e_quant()
        Q_o1(2, 0, 2)
        e_work(eb, 4)
        e_quant()
        P2s(3, (0, 1), "a")
        T_o1(2, 1)
        P2s(3, (2, 3), "a")
        P3(1, 2, 0)
        P3(1, 3, 0)
        Q_o1(2, 2, 2)
        T_o1(3, 0)
        P3(1, 0, 1)
        Q_o1(3, 0, 2)
        P3(1, 1, 1)
        T_o1(3, 1)
        P3(0, 0, 0)
        P3(0, 0, 1)
        Q_o1(3, 2, 2)
        P3(0, 1, 0)
        P3(0, 1, 1)
        P3(1, 2, 1)
        P3(1, 3, 1)
        P3(0, 2, 0)
        P3(0, 2, 1)
        P3(0, 3, 0)
        P3(0, 3, 1)
